import numpy as np
CORES = [3,11,19,27,35,43,51,59,67,75,83,91,131,139,147,155]
N = 16
def setup_inputs(rng):
    return {"x1": rng.standard_normal((N, 128, 16), dtype=np.float32), "x2": rng.standard_normal((N, 128, 128), dtype=np.float32)}
def reference(x1, x2):
    out = []
    s = x1.sum(axis=0, dtype=np.float64).astype(x1.dtype)
    b = 16 // N
    out.append(np.stack([s[:, r * b:(r + 1) * b] for r in range(N)]))
    g = np.concatenate(list(x2), axis=1)
    out.append(np.broadcast_to(g, (N,) + g.shape))
    return {"y1": out[0], "y2": out[1]}

@@ -1,0 +1,154 @@
+from concourse.bass import DstId, RemoteDMATransfer
+
+N = 16
+NPAIR = 8
+RCORE = 3
+F_OFFS = [1, 2, 3, 4, 5]
+F_CORE = [6, 2, 7, 6, 2]
+OWN_ROUTE = {4: [6, 7]}
+MATE_ROUTE = {5: [6, 7]}
+LOCAL_BY = 5
+ARCS = [[1, 2], [6, 7, 0], [3, 4], [5]]
+ROOTS = [103, 111, 119, 127]
+RS_FIRST = False
+ON = 0xFF00
+OFF = 0x00FF
+
+SCRATCH = {
+    "own": ("dram", [128, 128], "float32"),
+    "hb": ("dram", [2, 128, 128], "float32"),
+    "land": ("sbuf", [128, 2048], "float32"),
+    "x1s": ("dram", [128, 16], "float32"),
+    "x1l": ("dram", [16, 128, 16], "float32"),
+    "ssum": ("dram", [128, 16], "float32"),
+}
+SEMAPHORES = ["b%d" % j for j in range(N)] + ["ld1", "ld2", "ldl", "st", "y1s", "sent", "xa", "rs"]
+
+
+def f_slot(k):
+    return sum(1 for i in range(k) if F_CORE[i] == F_CORE[k])
+
+
+def root_ranks(i):
+    par = (ROOTS[i] // 8) % 2
+    same = [k for k in range(len(ROOTS)) if (ROOTS[k] // 8) % 2 == par]
+    if len(same) == len(ROOTS):
+        ranks = list(range(N))
+    else:
+        ranks = [r for r in range(N) if r % 2 == par]
+    n = len(ranks) // len(same)
+    p = same.index(i)
+    return ranks[p * n:(p + 1) * n]
+
+
+def rank_program(g, core, T, topo):
+    cores = list(T.cores)
+    sem = T.sem
+
+    def on_chip(rank, k):
+        return cores[rank] - RCORE + k
+
+    def did(d):
+        rid, pid = topo.addr(d, core)
+        return DstId(rid=rid, pnc=pid)
+
+    def copy(src, dsts, mask, s):
+        return RemoteDMATransfer(dst_ids=[did(d) for d, ap in dsts], dma_engine_mask=mask, remote_sem=s,
+                                 srcs=[src], dsts=[ap for d, ap in dsts], alu_op=0)
+
+    def cols(j):
+        return T.land[:, 128 * j:128 * (j + 1)]
+
+    def send(transfers):
+        transfers = [t for t in transfers if t is not None]
+        g.remote_dma_fused(transfers, local_sem=sem.sent)
+        return 8 * len(transfers)
+
+    if core in ROOTS:
+        ranks = root_ranks(ROOTS.index(core))
+        g.wait_ge(sem.xa, 8 * N)
+        g.remote_dma_fused([RemoteDMATransfer(dst_ids=[did(cores[r]) for r in ranks], dma_engine_mask=OFF, remote_sem=sem.rs,
+                                              srcs=[T.x1l[i] for i in range(N)], dsts=[T.ssum[:] for r in ranks], alu_op=1)],
+                           local_sem=sem.sent)
+        g.wait_ge(sem.sent, 8)
+        return
+
+    here = [r for r in range(N) if cores[r] // 8 == core // 8]
+    if not here:
+        return
+    me = here[0]
+    a, q = me // 2, me % 2
+    k = core % 8
+
+    def peer(t):
+        return 2 * ((a + t) % NPAIR) + q
+
+    if k != RCORE:
+        sent = 0
+        if k in F_CORE:
+            for i, t in enumerate(F_OFFS):
+                if F_CORE[i] != k:
+                    continue
+                j = peer(-t)
+                g.wait_ge(sem["b%d" % j], 8)
+                src = T.hb[f_slot(i)]
+                sent += send([copy(src, [(cores[me ^ 1], cols(j))], OFF, sem["b%d" % j]),
+                              copy(src, [(cores[me], cols(j))], ON, sem["b%d" % j])])
+        elif k in OWN_ROUTE or k in MATE_ROUTE:
+            j = me if k in OWN_ROUTE else me ^ 1
+            offs = OWN_ROUTE[k] if k in OWN_ROUTE else MATE_ROUTE[k]
+            g.wait_ge(sem["b%d" % j], 8)
+            sent += send([copy(T.hb[0], [(cores[peer(t)], cols(j)) for t in offs], OFF, sem["b%d" % j]),
+                          copy(T.hb[0], [(cores[me], cols(j))], ON, sem["b%d" % j]) if k == LOCAL_BY else None])
+        if sent:
+            g.wait_ge(sem.sent, sent)
+        return
+
+    bme = sem["b%d" % me]
+    g.sync.dma_start(T.own[:], T.x2[:]).then_inc(sem.ld2, 16)
+    g.scalar.dma_start(T.x1s[:], T.x1[:]).then_inc(sem.ld1, 16)
+    g.scalar.wait_ge(sem.ld2, 16)
+    g.scalar.dma_start(cols(me), T.x2[:]).then_inc(sem.ldl, 16)
+
+    sent = 0
+
+    def send_x1():
+        g.wait_ge(sem.ld1, 16)
+        return send([copy(T.x1s[:], [(d, T.x1l[me]) for d in ROOTS], OFF, sem.xa)])
+
+    if RS_FIRST:
+        sent += send_x1()
+    g.wait_ge(sem.ld2, 16)
+    off = [(on_chip(me ^ 1, h), T.hb[0]) for h in MATE_ROUTE]
+    off += [(on_chip(peer(t), F_CORE[i]), T.hb[f_slot(i)]) for i, t in enumerate(F_OFFS)]
+    on = [(on_chip(me, h), T.hb[0]) for h in OWN_ROUTE]
+    sent += send([copy(T.own[:], off, OFF, bme), copy(T.own[:], on, ON, bme) if on else None])
+    if not RS_FIRST:
+        sent += send_x1()
+
+    queues = [g.sync, g.scalar]
+    stores = 0
+    for n, arc in enumerate(ARCS):
+        qu = queues[n % 2]
+        pairs = sorted((a - t) % NPAIR for t in arc)
+        for p in pairs:
+            for j in (2 * p, 2 * p + 1):
+                if j == me:
+                    qu.wait_ge(sem.ldl, 16)
+                else:
+                    qu.wait_ge(sem["b%d" % j], 8)
+        runs = []
+        for p in pairs:
+            if runs and runs[-1][1] == p:
+                runs[-1][1] = p + 1
+            else:
+                runs.append([p, p + 1])
+        for lo, hi in runs:
+            qu.dma_start(T.y2[:, 256 * lo:256 * hi], T.land[:, 256 * lo:256 * hi]).then_inc(sem.st, 16)
+            stores += 1
+
+    g.wait_ge(sem.rs, 8)
+    g.dma_start(T.y1[:], T.ssum[:, me:me + 1], allow_slow_non_contiguous=True).then_inc(sem.y1s, 16)
+    g.wait_ge(sem.y1s, 16)
+    g.wait_ge(sem.sent, sent)
+    g.wait_ge(sem.st, 16 * stores)

@@ -5,18 +5,20 @@ NPAIR = 8
 RCORE = 3
 F_OFFS = [1, 2, 3, 4, 5]
 F_CORE = [6, 2, 7, 6, 2]
+D_OFFS = []
 OWN_ROUTE = {4: [6, 7]}
 MATE_ROUTE = {5: [6, 7]}
 LOCAL_BY = 5
 ARCS = [[1, 2], [6, 7, 0], [3, 4], [5]]
 ROOTS = [103, 111, 119, 127]
-RS_FIRST = False
+RS_FIRST = True
 ON = 0xFF00
 OFF = 0x00FF
 
 SCRATCH = {
     "own": ("dram", [128, 128], "float32"),
     "hb": ("dram", [2, 128, 128], "float32"),
+    "dl": ("dram", [4, 128, 128], "float32"),
     "land": ("sbuf", [128, 2048], "float32"),
     "x1s": ("dram", [128, 16], "float32"),
     "x1l": ("dram", [16, 128, 16], "float32"),
@@ -121,22 +123,23 @@ def rank_program(g, core, T, topo):
     g.wait_ge(sem.ld2, 16)
     off = [(on_chip(me ^ 1, h), T.hb[0]) for h in MATE_ROUTE]
     off += [(on_chip(peer(t), F_CORE[i]), T.hb[f_slot(i)]) for i, t in enumerate(F_OFFS)]
+    for i, t in enumerate(D_OFFS):
+        off += [(cores[peer(t)], T.dl[2 * i]), (cores[peer(t) ^ 1], T.dl[2 * i + 1])]
     on = [(on_chip(me, h), T.hb[0]) for h in OWN_ROUTE]
     sent += send([copy(T.own[:], off, OFF, bme), copy(T.own[:], on, ON, bme) if on else None])
     if not RS_FIRST:
         sent += send_x1()
 
-    queues = [g.sync, g.scalar]
-    stores = 0
-    for n, arc in enumerate(ARCS):
-        qu = queues[n % 2]
+    jobs = []
+    for arc in ARCS:
+        if arc[0] in D_OFFS:
+            for t in arc:
+                j = peer(-t)
+                i = D_OFFS.index(t)
+                jobs.append(([j], 128 * j, 128 * (j + 1), T.dl[2 * i]))
+                jobs.append(([j ^ 1], 128 * (j ^ 1), 128 * ((j ^ 1) + 1), T.dl[2 * i + 1]))
+            continue
         pairs = sorted((a - t) % NPAIR for t in arc)
-        for p in pairs:
-            for j in (2 * p, 2 * p + 1):
-                if j == me:
-                    qu.wait_ge(sem.ldl, 16)
-                else:
-                    qu.wait_ge(sem["b%d" % j], 8)
         runs = []
         for p in pairs:
             if runs and runs[-1][1] == p:
@@ -144,11 +147,19 @@ def rank_program(g, core, T, topo):
             else:
                 runs.append([p, p + 1])
         for lo, hi in runs:
-            qu.dma_start(T.y2[:, 256 * lo:256 * hi], T.land[:, 256 * lo:256 * hi]).then_inc(sem.st, 16)
-            stores += 1
+            jobs.append((list(range(2 * lo, 2 * hi)), 256 * lo, 256 * hi, T.land[:, 256 * lo:256 * hi]))
+    queues = [g.sync, g.scalar]
+    for n, (blocks, c0, c1, src) in enumerate(jobs):
+        qu = queues[n % 2]
+        for j in blocks:
+            if j == me:
+                qu.wait_ge(sem.ldl, 16)
+            else:
+                qu.wait_ge(sem["b%d" % j], 8)
+        qu.dma_start(T.y2[:, c0:c1], src).then_inc(sem.st, 16)
 
     g.wait_ge(sem.rs, 8)
     g.dma_start(T.y1[:], T.ssum[:, me:me + 1], allow_slow_non_contiguous=True).then_inc(sem.y1s, 16)
     g.wait_ge(sem.y1s, 16)
     g.wait_ge(sem.sent, sent)
-    g.wait_ge(sem.st, 16 * stores)
+    g.wait_ge(sem.st, 16 * len(jobs))

@@ -5,42 +5,29 @@ NPAIR = 8
 RCORE = 3
 F_OFFS = [1, 2, 3, 4, 5]
 F_CORE = [6, 2, 7, 6, 2]
-D_OFFS = []
 OWN_ROUTE = {4: [6, 7]}
 MATE_ROUTE = {5: [6, 7]}
 LOCAL_BY = 5
 ARCS = [[1, 2], [6, 7, 0], [3, 4], [5]]
-ROOTS = [103, 111, 119, 127]
-RS_FIRST = True
+ROOTS = [103, 111, 119, 127, 231, 239, 247, 255]
+NR = 8
+W = 16 // NR
 ON = 0xFF00
 OFF = 0x00FF
 
 SCRATCH = {
     "own": ("dram", [128, 128], "float32"),
     "hb": ("dram", [2, 128, 128], "float32"),
-    "dl": ("dram", [4, 128, 128], "float32"),
     "land": ("sbuf", [128, 2048], "float32"),
-    "x1s": ("dram", [128, 16], "float32"),
-    "x1l": ("dram", [16, 128, 16], "float32"),
-    "ssum": ("dram", [128, 16], "float32"),
+    "x1s": ("dram", [NR, 128, W], "float32"),
+    "x1l": ("dram", [16, 128, W], "float32"),
+    "ssum": ("dram", [NR, 128, W], "float32"),
 }
 SEMAPHORES = ["b%d" % j for j in range(N)] + ["ld1", "ld2", "ldl", "st", "y1s", "sent", "xa", "rs"]
 
 
 def f_slot(k):
     return sum(1 for i in range(k) if F_CORE[i] == F_CORE[k])
-
-
-def root_ranks(i):
-    par = (ROOTS[i] // 8) % 2
-    same = [k for k in range(len(ROOTS)) if (ROOTS[k] // 8) % 2 == par]
-    if len(same) == len(ROOTS):
-        ranks = list(range(N))
-    else:
-        ranks = [r for r in range(N) if r % 2 == par]
-    n = len(ranks) // len(same)
-    p = same.index(i)
-    return ranks[p * n:(p + 1) * n]
 
 
 def rank_program(g, core, T, topo):
@@ -67,10 +54,10 @@ def rank_program(g, core, T, topo):
         return 8 * len(transfers)
 
     if core in ROOTS:
-        ranks = root_ranks(ROOTS.index(core))
-        g.wait_ge(sem.xa, 8 * N)
-        g.remote_dma_fused([RemoteDMATransfer(dst_ids=[did(cores[r]) for r in ranks], dma_engine_mask=OFF, remote_sem=sem.rs,
-                                              srcs=[T.x1l[i] for i in range(N)], dsts=[T.ssum[:] for r in ranks], alu_op=1)],
+        kr = ROOTS.index(core)
+        g.wait_ge(sem.xa, N)
+        g.remote_dma_fused([RemoteDMATransfer(dst_ids=[did(c) for c in cores], dma_engine_mask=OFF, remote_sem=sem.rs,
+                                              srcs=[T.x1l[i] for i in range(N)], dsts=[T.ssum[kr] for c in cores], alu_op=1)],
                            local_sem=sem.sent)
         g.wait_ge(sem.sent, 8)
         return
@@ -107,59 +94,43 @@ def rank_program(g, core, T, topo):
         return
 
     bme = sem["b%d" % me]
-    g.sync.dma_start(T.own[:], T.x2[:]).then_inc(sem.ld2, 16)
     g.scalar.dma_start(T.x1s[:], T.x1[:]).then_inc(sem.ld1, 16)
+    g.sync.dma_start(T.own[:], T.x2[:]).then_inc(sem.ld2, 16)
     g.scalar.wait_ge(sem.ld2, 16)
     g.scalar.dma_start(cols(me), T.x2[:]).then_inc(sem.ldl, 16)
 
     sent = 0
+    g.wait_ge(sem.ld1, 16)
+    g.remote_dma_fused([copy(T.x1s[i], [(ROOTS[i], T.x1l[me])], 1 << i, sem.xa) for i in range(NR)], local_sem=sem.sent)
+    sent += NR
 
-    def send_x1():
-        g.wait_ge(sem.ld1, 16)
-        return send([copy(T.x1s[:], [(d, T.x1l[me]) for d in ROOTS], OFF, sem.xa)])
-
-    if RS_FIRST:
-        sent += send_x1()
     g.wait_ge(sem.ld2, 16)
     off = [(on_chip(me ^ 1, h), T.hb[0]) for h in MATE_ROUTE]
     off += [(on_chip(peer(t), F_CORE[i]), T.hb[f_slot(i)]) for i, t in enumerate(F_OFFS)]
-    for i, t in enumerate(D_OFFS):
-        off += [(cores[peer(t)], T.dl[2 * i]), (cores[peer(t) ^ 1], T.dl[2 * i + 1])]
     on = [(on_chip(me, h), T.hb[0]) for h in OWN_ROUTE]
     sent += send([copy(T.own[:], off, OFF, bme), copy(T.own[:], on, ON, bme) if on else None])
-    if not RS_FIRST:
-        sent += send_x1()
 
     jobs = []
     for arc in ARCS:
-        if arc[0] in D_OFFS:
-            for t in arc:
-                j = peer(-t)
-                i = D_OFFS.index(t)
-                jobs.append(([j], 128 * j, 128 * (j + 1), T.dl[2 * i]))
-                jobs.append(([j ^ 1], 128 * (j ^ 1), 128 * ((j ^ 1) + 1), T.dl[2 * i + 1]))
-            continue
-        pairs = sorted((a - t) % NPAIR for t in arc)
         runs = []
-        for p in pairs:
+        for p in sorted((a - t) % NPAIR for t in arc):
             if runs and runs[-1][1] == p:
                 runs[-1][1] = p + 1
             else:
                 runs.append([p, p + 1])
-        for lo, hi in runs:
-            jobs.append((list(range(2 * lo, 2 * hi)), 256 * lo, 256 * hi, T.land[:, 256 * lo:256 * hi]))
+        jobs += runs
     queues = [g.sync, g.scalar]
-    for n, (blocks, c0, c1, src) in enumerate(jobs):
+    for n, (lo, hi) in enumerate(jobs):
         qu = queues[n % 2]
-        for j in blocks:
+        for j in range(2 * lo, 2 * hi):
             if j == me:
                 qu.wait_ge(sem.ldl, 16)
             else:
                 qu.wait_ge(sem["b%d" % j], 8)
-        qu.dma_start(T.y2[:, c0:c1], src).then_inc(sem.st, 16)
+        qu.dma_start(T.y2[:, 256 * lo:256 * hi], T.land[:, 256 * lo:256 * hi]).then_inc(sem.st, 16)
 
-    g.wait_ge(sem.rs, 8)
-    g.dma_start(T.y1[:], T.ssum[:, me:me + 1], allow_slow_non_contiguous=True).then_inc(sem.y1s, 16)
+    g.wait_ge(sem.rs, 8 * NR)
+    g.dma_start(T.y1[:], T.ssum[:, me // W::16 // W, me % W:me % W + 1], allow_slow_non_contiguous=True).then_inc(sem.y1s, 16)
     g.wait_ge(sem.y1s, 16)
     g.wait_ge(sem.sent, sent)
     g.wait_ge(sem.st, 16 * len(jobs))

@@ -10,8 +10,9 @@ MATE_ROUTE = {5: [6, 7]}
 LOCAL_BY = 5
 ARCS = [[1, 2], [6, 7, 0], [3, 4], [5]]
 ROOTS = [103, 111, 119, 127, 231, 239, 247, 255]
-NR = 8
+NR = 4
 W = 16 // NR
+EP = 8 // NR
 ON = 0xFF00
 OFF = 0x00FF
 
@@ -55,9 +56,10 @@ def rank_program(g, core, T, topo):
 
     if core in ROOTS:
         kr = ROOTS.index(core)
-        g.wait_ge(sem.xa, N)
-        g.remote_dma_fused([RemoteDMATransfer(dst_ids=[did(c) for c in cores], dma_engine_mask=OFF, remote_sem=sem.rs,
-                                              srcs=[T.x1l[i] for i in range(N)], dsts=[T.ssum[kr] for c in cores], alu_op=1)],
+        mine = [cores[r] for r in range(N) if r % 2 == kr % 2]
+        g.wait_ge(sem.xa, EP * N)
+        g.remote_dma_fused([RemoteDMATransfer(dst_ids=[did(c) for c in mine], dma_engine_mask=OFF, remote_sem=sem.rs,
+                                              srcs=[T.x1l[i] for i in range(N)], dsts=[T.ssum[kr // 2] for c in mine], alu_op=1)],
                            local_sem=sem.sent)
         g.wait_ge(sem.sent, 8)
         return
@@ -101,8 +103,9 @@ def rank_program(g, core, T, topo):
 
     sent = 0
     g.wait_ge(sem.ld1, 16)
-    g.remote_dma_fused([copy(T.x1s[i], [(ROOTS[i], T.x1l[me])], 1 << i, sem.xa) for i in range(NR)], local_sem=sem.sent)
-    sent += NR
+    g.remote_dma_fused([copy(T.x1s[i], [(ROOTS[2 * i + q], T.x1l[me]), (ROOTS[2 * i + 1 - q], T.x1l[me])],
+                             ((1 << EP) - 1) << (EP * i), sem.xa) for i in range(NR)], local_sem=sem.sent)
+    sent += 8
 
     g.wait_ge(sem.ld2, 16)
     off = [(on_chip(me ^ 1, h), T.hb[0]) for h in MATE_ROUTE]

from concourse.bass import DstId, RemoteDMATransfer

N = 16
NPAIR = 8
RCORE = 3
F_OFFS = [1, 2, 3, 4, 5]
F_CORE = [6, 2, 7, 6, 2]
OWN_ROUTE = {4: [6, 7]}
MATE_ROUTE = {5: [6, 7]}
LOCAL_BY = 5
ARCS = [[1, 2], [6, 7, 0], [3, 4], [5]]
ROOTS = [103, 111, 119, 127, 231, 239, 247, 255]
NR = 4
W = 16 // NR
EP = 8 // NR
ON = 0xFF00
OFF = 0x00FF

SCRATCH = {
    "own": ("dram", [128, 128], "float32"),
    "hb": ("dram", [2, 128, 128], "float32"),
    "land": ("sbuf", [128, 2048], "float32"),
    "x1s": ("dram", [NR, 128, W], "float32"),
    "x1l": ("dram", [16, 128, W], "float32"),
    "ssum": ("dram", [NR, 128, W], "float32"),
}
SEMAPHORES = ["b%d" % j for j in range(N)] + ["ld1", "ld2", "ldl", "st", "y1s", "sent", "xa", "rs"]


def f_slot(k):
    return sum(1 for i in range(k) if F_CORE[i] == F_CORE[k])


def rank_program(g, core, T, topo):
    cores = list(T.cores)
    sem = T.sem

    def on_chip(rank, k):
        return cores[rank] - RCORE + k

    def did(d):
        rid, pid = topo.addr(d, core)
        return DstId(rid=rid, pnc=pid)

    def copy(src, dsts, mask, s):
        return RemoteDMATransfer(dst_ids=[did(d) for d, ap in dsts], dma_engine_mask=mask, remote_sem=s,
                                 srcs=[src], dsts=[ap for d, ap in dsts], alu_op=0)

    def cols(j):
        return T.land[:, 128 * j:128 * (j + 1)]

    def send(transfers):
        transfers = [t for t in transfers if t is not None]
        g.remote_dma_fused(transfers, local_sem=sem.sent)
        return 8 * len(transfers)

    if core in ROOTS:
        kr = ROOTS.index(core)
        mine = [cores[r] for r in range(N) if r % 2 == kr % 2]
        g.wait_ge(sem.xa, EP * N)
        g.remote_dma_fused([RemoteDMATransfer(dst_ids=[did(c) for c in mine], dma_engine_mask=OFF, remote_sem=sem.rs,
                                              srcs=[T.x1l[i] for i in range(N)], dsts=[T.ssum[kr // 2] for c in mine], alu_op=1)],
                           local_sem=sem.sent)
        g.wait_ge(sem.sent, 8)
        return

    here = [r for r in range(N) if cores[r] // 8 == core // 8]
    if not here:
        return
    me = here[0]
    a, q = me // 2, me % 2
    k = core % 8

    def peer(t):
        return 2 * ((a + t) % NPAIR) + q

    if k != RCORE:
        sent = 0
        if k in F_CORE:
            for i, t in enumerate(F_OFFS):
                if F_CORE[i] != k:
                    continue
                j = peer(-t)
                g.wait_ge(sem["b%d" % j], 8)
                src = T.hb[f_slot(i)]
                sent += send([copy(src, [(cores[me ^ 1], cols(j))], OFF, sem["b%d" % j]),
                              copy(src, [(cores[me], cols(j))], ON, sem["b%d" % j])])
        elif k in OWN_ROUTE or k in MATE_ROUTE:
            j = me if k in OWN_ROUTE else me ^ 1
            offs = OWN_ROUTE[k] if k in OWN_ROUTE else MATE_ROUTE[k]
            g.wait_ge(sem["b%d" % j], 8)
            sent += send([copy(T.hb[0], [(cores[peer(t)], cols(j)) for t in offs], OFF, sem["b%d" % j]),
                          copy(T.hb[0], [(cores[me], cols(j))], ON, sem["b%d" % j]) if k == LOCAL_BY else None])
        if sent:
            g.wait_ge(sem.sent, sent)
        return

    bme = sem["b%d" % me]
    g.scalar.dma_start(T.x1s[:], T.x1[:]).then_inc(sem.ld1, 16)
    g.sync.dma_start(T.own[:], T.x2[:]).then_inc(sem.ld2, 16)
    g.scalar.wait_ge(sem.ld2, 16)
    g.scalar.dma_start(cols(me), T.x2[:]).then_inc(sem.ldl, 16)

    sent = 0
    g.wait_ge(sem.ld1, 16)
    g.remote_dma_fused([copy(T.x1s[i], [(ROOTS[2 * i + q], T.x1l[me]), (ROOTS[2 * i + 1 - q], T.x1l[me])],
                             ((1 << EP) - 1) << (EP * i), sem.xa) for i in range(NR)], local_sem=sem.sent)
    sent += 8

    g.wait_ge(sem.ld2, 16)
    off = [(on_chip(me ^ 1, h), T.hb[0]) for h in MATE_ROUTE]
    off += [(on_chip(peer(t), F_CORE[i]), T.hb[f_slot(i)]) for i, t in enumerate(F_OFFS)]
    on = [(on_chip(me, h), T.hb[0]) for h in OWN_ROUTE]
    sent += send([copy(T.own[:], off, OFF, bme), copy(T.own[:], on, ON, bme) if on else None])

    jobs = []
    for arc in ARCS:
        runs = []
        for p in sorted((a - t) % NPAIR for t in arc):
            if runs and runs[-1][1] == p:
                runs[-1][1] = p + 1
            else:
                runs.append([p, p + 1])
        jobs += runs
    queues = [g.sync, g.scalar]
    for n, (lo, hi) in enumerate(jobs):
        qu = queues[n % 2]
        for j in range(2 * lo, 2 * hi):
            if j == me:
                qu.wait_ge(sem.ldl, 16)
            else:
                qu.wait_ge(sem["b%d" % j], 8)
        qu.dma_start(T.y2[:, 256 * lo:256 * hi], T.land[:, 256 * lo:256 * hi]).then_inc(sem.st, 16)

    g.wait_ge(sem.rs, 8 * NR)
    g.dma_start(T.y1[:], T.ssum[:, me // W::16 // W, me % W:me % W + 1], allow_slow_non_contiguous=True).then_inc(sem.y1s, 16)
    g.wait_ge(sem.y1s, 16)
    g.wait_ge(sem.sent, sent)
    g.wait_ge(sem.st, 16 * len(jobs))
